import numpy as np
import ml_dtypes


def mxq(x, axis, fmt="e4m3"):
    dtype, down = {"e4m3": (ml_dtypes.float8_e4m3fn, 7), "e5m2": (ml_dtypes.float8_e5m2, 14)}[fmt]
    v = np.moveaxis(np.asarray(x, np.float32).astype(ml_dtypes.bfloat16).astype(np.float64), axis, -1)
    blocks = v.reshape(v.shape[:-1] + (-1, 32))
    amax = np.abs(blocks).max(-1, keepdims=True)
    byte = np.maximum(np.where(amax > 0, np.frexp(amax)[1] - 1 + 127, 0) - down, 1)
    scale = np.exp2(byte - 127.0)
    codes = (blocks / scale).astype(np.float32).astype(dtype).astype(np.float64)
    return np.moveaxis((codes * scale).reshape(v.shape), -1, axis)


WIDE = False


def mx_kscale(k):
    if not WIDE:
        return np.ones(k)
    levels = np.array([10, -10, 5, -5, 0])
    if k % 512:
        return np.exp2(np.random.permutation(np.resize(levels, k // 32))).repeat(32)
    a = np.empty((k // 512, 16))
    for p in range(k // 512):
        a[p, :8] = np.random.permutation(np.resize(levels, 8))
        for g in range(8):
            far = levels[np.abs(levels - a[p, g]) >= 10]
            a[p, g + 8] = far[np.random.randint(len(far))]
    return np.exp2(a.ravel()).repeat(32)


def f64(x):
    return np.asarray(x).astype(np.float64)


def striped(idx):
    return np.tile(idx.reshape(-1, 16).T, (8, 1)).astype(np.uint16)


def unstriped(offs):
    return offs[:16].T.reshape(-1).astype(np.int64)


E2M1 = np.array([0.0, 0.5, 1.0, 1.5, 2.0, 3.0, 4.0, 6.0, -0.0, -0.5, -1.0, -1.5, -2.0, -3.0, -4.0, -6.0])


def pack_weight(w, fmt):
    k, n = w.shape
    w = f64(np.asarray(w, np.float32).astype(ml_dtypes.bfloat16)).reshape(k // 32, 32, n)
    amax = np.abs(w).max(1)
    if fmt == "e4m3":
        byte = np.frexp(amax)[1] - 1 + 127 - 7
    else:
        mant, ex = np.frexp(amax / 6.0)
        byte = np.where(mant > 0.5, ex, ex - 1) + 127
    byte = np.clip(np.where(amax > 0, byte, 1), 1, 254)
    scaled = (w * np.exp2(127.0 - byte)[:, None, :]).reshape(k, n).astype(np.float32)
    by_word = np.ascontiguousarray(scaled.reshape(k // 512, 128, 4, n).transpose(0, 1, 3, 2))
    if fmt == "e4m3":
        words = by_word.astype(ml_dtypes.float8_e4m3fn).view(np.uint8)
    else:
        c = by_word.astype(ml_dtypes.float4_e2m1fn).view(np.uint8) & 0xF
        words = (c[..., 0::2] | (c[..., 1::2] << 4)).reshape(k // 512, 128, 2 * n)
    return np.ascontiguousarray(words), np.ascontiguousarray(byte.astype(np.uint8).reshape(k // 512, 16, n))


def unpack_weight(words, scales, fmt):
    g, _, n = scales.shape
    words = np.ascontiguousarray(words).reshape(g, 128, n, -1)
    if fmt == "e4m3":
        vals = words.view(ml_dtypes.float8_e4m3fn).astype(np.float64)
    else:
        nib = np.empty((g, 128, n, 4), np.uint8)
        nib[..., 0::2] = words & 0xF
        nib[..., 1::2] = words >> 4
        vals = E2M1[nib]
    vals = vals * np.repeat(np.exp2(scales.astype(np.float64) - 127.0), 8, axis=1)[..., None]
    return vals.transpose(0, 1, 3, 2).reshape(g * 512, n)


def gelu(v):
    return 0.5 * v * (1.0 + np.tanh(np.sqrt(2.0 / np.pi) * (v + 0.044715 * v**3)))


K, H, N, T, S = 512, 1024, 512, 4096, 1024

def setup_inputs():
    n = np.random.standard_normal
    s = mx_kscale(K)[:, None]
    u = mx_kscale(H)[:, None]
    tab_words, tab_scales = pack_weight(n((K, T)) * s, "e2m1")
    wm_words, wm_scales = pack_weight(n((K, H)) / np.sqrt(K) / s * u.T, "e4m3")
    wo_words, wo_scales = pack_weight(n((H, N)) / np.sqrt(H) / u, "e2m1")
    return {
        "tab_words": tab_words, "tab_scales": tab_scales,
        "offs": striped(np.random.permutation(T)[:S]),
        "offs2": striped(np.random.permutation(T)[:S]),
        "wg": (n((K, H)) / np.sqrt(K) / s).astype(np.float32),
        "bg": (0.5 * n(H)).astype(np.float32),
        "wm_words": wm_words, "wm_scales": wm_scales,
        "wh": (n((K, H)) / np.sqrt(K) / s * u.T).astype(np.float32),
        "wo_words": wo_words, "wo_scales": wo_scales,
        "bo": (0.5 * n(N)).astype(np.float32),
    }

def reference(tab_words, tab_scales, offs, offs2, wg, bg, wm_words, wm_scales, wh, wo_words, wo_scales, bo):
    TW = unpack_weight(tab_words, tab_scales, "e2m1")
    v = TW[:, unstriped(offs)]
    v2 = TW[:, unstriped(offs2)]
    gp = mxq(f64(wg), 0, "e4m3").T @ v
    gate = 1.0 / (1.0 + np.exp(-(gp + f64(bg)[:, None])))
    mod = unpack_weight(wm_words, wm_scales, "e4m3").T @ v
    head = mxq(f64(wh), 0, "e4m3").T @ v2
    h = head + gate * (mod - head)
    y = unpack_weight(wo_words, wo_scales, "e2m1").T @ mxq(h, 0, "e4m3")
    return y + f64(bo)[:, None]

@@ -1,0 +1,306 @@
+from contextlib import ExitStack
+
+import concourse.mybir as mybir
+
+K, H, N, T, S = 512, 1024, 512, 4096, 1024
+FLOPS = 2 * K * H * S * 3 + 2 * H * N * S
+
+F32 = mybir.dt.float32
+BF16 = mybir.dt.bfloat16
+I32 = mybir.dt.int32
+U32 = mybir.dt.uint32
+U16 = mybir.dt.uint16
+U8 = mybir.dt.uint8
+FP8X4 = mybir.dt.float8_e4m3fn_x4
+FP4X4 = mybir.dt.float4_e2m1fn_x4
+ACT = mybir.ActivationFunctionType
+ALU = mybir.AluOpType
+
+P = 128
+PACK = 4
+BANK = 512
+PIECE = 128
+PASSES = H // (P * PACK)
+CHUNKS = S // BANK
+REPEATED = frozenset([(0, 1, 0), (1, 0, 3)])
+ADD_ON_GPSIMD = frozenset()
+TAIL_ON_VECTOR = (3,)
+WARM = True
+
+
+def tile_list_compound_gate_features_kernel(
+    tc, tab_words, tab_scales, offs, offs2, wg, bg, wm_words, wm_scales, wh, wo_words, wo_scales, bo, out
+):
+    nc = tc.nc
+    with ExitStack() as ctx:
+        lists = ctx.enter_context(tc.tile_pool(name="lists", bufs=1))
+        keep = ctx.enter_context(tc.tile_pool(name="keep", bufs=1))
+        work = ctx.enter_context(tc.tile_pool(name="work", bufs=2))
+        psum = ctx.enter_context(tc.psum_pool(name="psum", bufs=2))
+
+        mod_list = lists.tile([P, S // 16], U16, name="mod_list")
+        head_list = lists.tile([P, S // 16], U16, name="head_list")
+        nc.sync.dma_start(mod_list[:], offs)
+
+        table_words = keep.tile([P, T], U16, name="table_words", align_bytes=64)
+        table_scales = keep.tile([P, T], U8, name="table_scales", align_bytes=64)
+        wm_raw_scales = keep.tile([P, H], U8, name="wm_raw_scales", align_bytes=64)
+        wo_codes = keep.tile([P, PASSES, 2 * N], U8, name="wo_codes", align_bytes=64)
+        wo_plane = keep.tile([P, PASSES, N], U8, name="wo_plane", align_bytes=64)
+        bg_cols = keep.tile([P, PASSES, PACK], F32, name="bg_cols")
+        bo_cols = keep.tile([P, N // P], F32, name="bo_cols")
+
+        nc.vector.memset(table_scales[:].bitcast(I32), 0)
+        nc.gpsimd.memset(wm_raw_scales[:].bitcast(I32), 0)
+        nc.gpsimd.memset(wo_plane[:].rearrange("p a c -> p (a c)").bitcast(I32), 0)
+        if WARM:
+            warm_in = keep.tile([P, 1], F32, name="warm_in")
+            warm_out = keep.tile([P, 1], F32, name="warm_out")
+            nc.gpsimd.memset(warm_in[:], 0.0)
+            nc.scalar.activation(warm_out[:], warm_in[:], ACT.Sigmoid)
+
+        nc.sync.dma_start(table_words[:].bitcast(I32), tab_words[0].bitcast(I32))
+        for q in range(4):
+            nc.sync.dma_start(
+                table_scales[32 * q : 32 * q + 4, :].bitcast(I32), tab_scales[0, 4 * q : 4 * q + 4, :].bitcast(I32)
+            )
+        with nc.allow_non_contiguous_dma(reason="biases, one short run a partition"):
+            nc.sync.dma_start(bg_cols[:], bg.rearrange("(a p t) -> p a t", a=PASSES, t=PACK))
+
+        def load_float_weight(w, a, name):
+            raw = keep.tile([P, PACK, BANK], F32, name=name)
+            nc.sync.dma_start(raw[:], w[:, BANK * a : BANK * (a + 1)].rearrange("(p j) c -> p j c", j=PACK))
+            return raw
+
+        def load_wm_words(a):
+            raw = keep.tile([P, BANK], I32, name="wm_raw%d" % a)
+            nc.sync.dma_start(
+                raw[:], wm_words[0].rearrange("p c i -> p (c i)")[:, 4 * BANK * a : 4 * BANK * (a + 1)].bitcast(I32)
+            )
+            return raw
+
+        wg_raw, wh_raw, wm_raw = [], [], []
+        for a in range(PASSES):
+            wg_raw.append(load_float_weight(wg, a, "wg_raw%d" % a))
+            wm_raw.append(load_wm_words(a))
+            if a == 0:
+                for q in range(4):
+                    nc.sync.dma_start(
+                        wm_raw_scales[32 * q : 32 * q + 4, :].bitcast(I32),
+                        wm_scales[0, 4 * q : 4 * q + 4, :].bitcast(I32),
+                    )
+            wh_raw.append(load_float_weight(wh, a, "wh_raw%d" % a))
+            if a == 0:
+                nc.sync.dma_start(head_list[:], offs2)
+        nc.sync.dma_start(wo_codes[:].bitcast(I32), wo_words.rearrange("a p c -> p a c").bitcast(I32))
+        for q in range(4):
+            nc.sync.dma_start(
+                wo_plane[32 * q : 32 * q + 4, :, :].bitcast(I32),
+                wo_scales[:, 4 * q : 4 * q + 4, :].rearrange("a r c -> r a c").bitcast(I32),
+            )
+
+        with nc.allow_non_contiguous_dma(reason="bias, one value a partition"):
+            nc.sync.dma_start(bo_cols[:], bo.rearrange("(n p) -> p n", p=P))
+
+        def gather(name, offsets):
+            words = keep.tile([P, S], U16, name=name + "_words", align_bytes=64)
+            scales = keep.tile([P, S], U8, name=name + "_scales", align_bytes=64)
+            return words, scales
+
+        v_mod = gather("v_mod", mod_list)
+        v_head = gather("v_head", head_list)
+        nc.vector.tensor_copy(v_mod[0][:], table_words[:].indirect(mod_list[:]))
+        nc.vector.tensor_copy(v_mod[1][:], table_scales[:].indirect(mod_list[:]))
+        nc.vector.tensor_copy(v_head[0][:], table_words[:].indirect(head_list[:]))
+        nc.vector.tensor_copy(v_head[1][:], table_scales[:].indirect(head_list[:]))
+
+        def operand(name):
+            codes = keep.tile([P, BANK], U32, name=name + "_codes", align_bytes=64)
+            scales = keep.tile([P, BANK], U8, name=name + "_plane", align_bytes=64)
+            return codes, scales
+
+        def round_weight(raw, sign, name):
+            rounded = keep.tile([P, BANK * PACK], BF16, name=name, align_bytes=64)
+            nc.scalar.activation(
+                rounded[:].rearrange("p (t m j) -> p m t j", t=PACK, j=PACK),
+                raw[:].rearrange("p j (m t) -> p m t j", t=PACK),
+                ACT.Copy,
+                scale=sign,
+            )
+            return rounded
+
+        def quantise(rounded, dst, cols):
+            codes, scales = dst
+            nc.vector.quantize_mx(
+                out=codes[:, cols].bitcast(FP8X4),
+                scales=scales[:, cols],
+                in_=rounded,
+            )
+
+        def reorder_wm(a):
+            codes, scales = operand("wm%d" % a)
+            nc.vector.tensor_copy(
+                codes[:].bitcast(I32).rearrange("p (t m e) -> p m t e", t=PACK, e=2),
+                wm_raw[a][:].rearrange("p (m e t) -> p m t e", t=PACK, e=2),
+            )
+            nc.vector.tensor_copy(
+                scales[:].rearrange("p (t m) -> p t m", t=PACK),
+                wm_raw_scales[:, BANK * a : BANK * (a + 1)].rearrange("p (m t) -> p t m", t=PACK),
+            )
+            return codes, scales
+
+        def prepare(a):
+            whole = slice(0, BANK)
+            g_op, h_op = operand("wg%d" % a), operand("wh%d" % a)
+            g_round = round_weight(wg_raw[a], 1.0, "wg_round%d" % a)
+            h_round = round_weight(wh_raw[a], -1.0, "wh_round%d" % a)
+            quantise(g_round[:], g_op, whole)
+            m_op = reorder_wm(a)
+            quantise(h_round[:], h_op, whole)
+            return g_op, m_op, h_op
+
+        def product(dst, weight, t, v, cols, start=True, stop=True):
+            rows = slice(P * t, P * (t + 1))
+            nc.tensor.matmul_mx(
+                out=dst,
+                lhsT=weight[0][:, rows].bitcast(FP8X4),
+                lhsT_scale=weight[1][:, rows],
+                rhs=v[0][:, cols].bitcast(FP4X4),
+                rhs_scale=v[1][:, cols],
+                start=start,
+                stop=stop,
+            )
+
+        def gate_of(weights, a, t, cols):
+            pre = psum.tile([P, BANK], F32, name="pre", tag="pre")
+            product(pre[:], weights[0], t, v_mod, cols)
+            gate = work.tile([P, BANK], F32, name="gate", tag="gate", bufs=6)
+            nc.scalar.activation(gate[:], pre[:], ACT.Sigmoid, bias=bg_cols[:, a, t : t + 1])
+            return gate
+
+        def gate_less_one_times(dst, gate, bank):
+            nc.vector.scalar_tensor_tensor(dst, gate[:], 1.0, bank[:], ALU.subtract, ALU.mult)
+
+        def difference(weights, t, cols):
+            bank = psum.tile([P, BANK], F32, name="diff", tag="head")
+            product(bank[:], weights[1], t, v_mod, cols, stop=False)
+            product(bank[:], weights[2], t, v_head, cols, start=False)
+            return bank
+
+        def terms(weights, a, c, t, first, second):
+            cols = slice(BANK * c, BANK * (c + 1))
+            gate = gate_of(weights, a, t, cols)
+            mod = psum.tile([P, BANK], F32, name="mod", tag="mod")
+            product(mod[:], weights[1], t, v_mod, cols)
+            if (a, c, t) in REPEATED:
+                diff = difference(weights, t, cols)
+                nc.scalar.copy(first[:, t, :], mod[:])
+                gate_less_one_times(second[:, t, :], gate, diff)
+            else:
+                less_head = psum.tile([P, BANK], F32, name="less_head", tag="head")
+                product(less_head[:], weights[2], t, v_head, cols)
+                nc.vector.tensor_tensor(first[:, t, :], gate[:], mod[:], ALU.mult)
+                gate_less_one_times(second[:, t, :], gate, less_head)
+
+        def pairs(ap):
+            return ap.rearrange("p t (c i) -> p c t i", i=2)
+
+        def add_and_round(engine, dst, first, second):
+            engine.tensor_tensor(dst.rearrange("p (c i t) -> p c t i", i=2, t=PACK), pairs(first), pairs(second), ALU.add)
+
+        def last_product(dst, n, h_ops, cols):
+            for a in range(PASSES):
+                nc.tensor.matmul_mx(
+                    out=dst,
+                    lhsT=wo_codes[:, a, 2 * P * n : 2 * P * (n + 1)].bitcast(FP4X4),
+                    lhsT_scale=wo_plane[:, a, P * n : P * (n + 1)],
+                    rhs=h_ops[a][0][:, cols].bitcast(FP8X4),
+                    rhs_scale=h_ops[a][1][:, cols],
+                    start=(a == 0),
+                    stop=(a == PASSES - 1),
+                )
+
+        out_rows = out.rearrange("(n p) j -> p n j", p=P)
+        h_ops = {}
+
+        def group_terms(weights, a, c):
+            first = work.tile([P, PACK, BANK], F32, name="first", tag="first")
+            second = work.tile([P, PACK, BANK], F32, name="second", tag="second")
+            for t in range(PACK):
+                terms(weights, a, c, t, first, second)
+            return first, second
+
+        def group_sum(a, c, first, second):
+            h_round = work.tile([P, BANK * PACK], BF16, name="h_round", tag="h_round", align_bytes=64)
+            for b in range(BANK // PIECE):
+                js = slice(PIECE * b, PIECE * (b + 1))
+                engine = nc.gpsimd if (a, c, b) in ADD_ON_GPSIMD else nc.vector
+                add_and_round(
+                    engine, h_round[:, PACK * PIECE * b : PACK * PIECE * (b + 1)], first[:, :, js], second[:, :, js]
+                )
+            return h_round
+
+        def group_quantise(a, c, h_round):
+            h_ops[(a, c)] = operand("h%d%d" % (a, c))
+            quantise(h_round[:], h_ops[(a, c)], slice(0, BANK))
+
+        def features_whole(c):
+            for n in range(N // P):
+                acc = psum.tile([P, BANK], F32, name="acc", tag="acc")
+                last_product(acc[:], n, [h_ops[(a, c)] for a in range(PASSES)], slice(0, BANK))
+                res = work.tile([P, BANK], F32, name="res", tag="res", bufs=4)
+                nc.scalar.activation(res[:], acc[:], ACT.Identity, bias=bo_cols[:, n : n + 1])
+                nc.sync.dma_start(out_rows[:, n, BANK * c : BANK * (c + 1)], res[:])
+
+        w0 = prepare(0)
+        t00 = group_terms(w0, 0, 0)
+        w1 = prepare(1)
+        t10 = group_terms(w1, 1, 0)
+        group_quantise(0, 0, group_sum(0, 0, *t00))
+        t01 = group_terms(w0, 0, 1)
+        group_quantise(1, 0, group_sum(1, 0, *t10))
+
+        a, c = PASSES - 1, CHUNKS - 1
+        cols = slice(BANK * c, BANK * (c + 1))
+        scaled = keep.tile([P, PACK, BANK], F32, name="scaled")
+        for t in range(PACK):
+            gate = gate_of(w1, a, t, cols)
+            gate_less_one_times(scaled[:, t, :], gate, difference(w1, t, cols))
+        features_whole(0)
+
+        def tail_sum(b):
+            js = slice(PIECE * b, PIECE * (b + 1))
+            h_piece = keep.tile([P, PASSES, PACK * PIECE], BF16, name="h_piece%d" % b, align_bytes=64)
+            engine = nc.gpsimd if (0, c, b) in ADD_ON_GPSIMD else nc.vector
+            add_and_round(engine, h_piece[:, 0, :], t01[0][:, :, js], t01[1][:, :, js])
+            mod = psum.tile([P, PACK, PIECE], F32, name="mod_piece", tag="mod")
+            for t in range(PACK):
+                product(mod[:, t, :], w1[1], t, v_mod, slice(BANK * c + PIECE * b, BANK * c + PIECE * (b + 1)))
+            add_and_round(nc.vector, h_piece[:, 1, :], scaled[:, :, js], mod[:])
+            return h_piece
+
+        def tail_features(b, h_piece):
+            codes = keep.tile([P, PASSES * PIECE], U32, name="h_tail_codes%d" % b, align_bytes=64)
+            scales = keep.tile([P, PASSES * PIECE], U8, name="h_tail_plane%d" % b, align_bytes=64)
+            quantise(h_piece[:].rearrange("p a x -> p (a x)"), (codes, scales), slice(0, PASSES * PIECE))
+            acc = psum.tile([P, N // P, PIECE], F32, name="acc_piece", tag="acc")
+            halves = [slice(PIECE * k, PIECE * (k + 1)) for k in range(PASSES)]
+            for n in range(N // P):
+                last_product(acc[:, n, :], n, [(codes[:, x], scales[:, x]) for x in halves], slice(0, PIECE))
+            res = keep.tile([P, N // P, PIECE], F32, name="res_piece%d" % b)
+            if b in TAIL_ON_VECTOR:
+                nc.vector.tensor_tensor(
+                    res[:], acc[:], bo_cols[:].unsqueeze(2).to_broadcast([P, N // P, PIECE]), ALU.add
+                )
+            else:
+                for n in range(N // P):
+                    nc.scalar.activation(res[:, n, :], acc[:, n, :], ACT.Identity, bias=bo_cols[:, n : n + 1])
+            nc.sync.dma_start(out_rows[:, :, BANK * c + PIECE * b : BANK * c + PIECE * (b + 1)], res[:])
+
+        pending = None
+        for b in range(BANK // PIECE):
+            piece = tail_sum(b)
+            if pending is not None:
+                tail_features(b - 1, pending)
+            pending = piece
+        tail_features(BANK // PIECE - 1, pending)

@@ -22,9 +22,10 @@ BANK = 512
 PIECE = 128
 PASSES = H // (P * PACK)
 CHUNKS = S // BANK
-REPEATED = frozenset([(0, 1, 0), (1, 0, 3)])
-ADD_ON_GPSIMD = frozenset()
+REPEATED = frozenset([(0, 0, 3), (1, 1, 3)])
+TAIL_GPSIMD = 2
 TAIL_ON_VECTOR = (3,)
+HELD = {(0, 1, BANK): "h_early_codes", (1, 3, BANK): "h_tail2"}
 WARM = True
 
 
@@ -40,7 +41,6 @@ def tile_list_compound_gate_features_kernel(
 
         mod_list = lists.tile([P, S // 16], U16, name="mod_list")
         head_list = lists.tile([P, S // 16], U16, name="head_list")
-        nc.sync.dma_start(mod_list[:], offs)
 
         table_words = keep.tile([P, T], U16, name="table_words", align_bytes=64)
         table_scales = keep.tile([P, T], U8, name="table_scales", align_bytes=64)
@@ -60,15 +60,14 @@ def tile_list_compound_gate_features_kernel(
             nc.scalar.activation(warm_out[:], warm_in[:], ACT.Sigmoid)
 
         nc.sync.dma_start(table_words[:].bitcast(I32), tab_words[0].bitcast(I32))
+        nc.sync.dma_start(mod_list[:], offs)
         for q in range(4):
             nc.sync.dma_start(
                 table_scales[32 * q : 32 * q + 4, :].bitcast(I32), tab_scales[0, 4 * q : 4 * q + 4, :].bitcast(I32)
             )
-        with nc.allow_non_contiguous_dma(reason="biases, one short run a partition"):
-            nc.sync.dma_start(bg_cols[:], bg.rearrange("(a p t) -> p a t", a=PASSES, t=PACK))
 
         def load_float_weight(w, a, name):
-            raw = keep.tile([P, PACK, BANK], F32, name=name)
+            raw = keep.tile([P, PACK, BANK], F32, name=name, tag=name, align_bytes=64)
             nc.sync.dma_start(raw[:], w[:, BANK * a : BANK * (a + 1)].rearrange("(p j) c -> p j c", j=PACK))
             return raw
 
@@ -89,9 +88,9 @@ def tile_list_compound_gate_features_kernel(
                         wm_raw_scales[32 * q : 32 * q + 4, :].bitcast(I32),
                         wm_scales[0, 4 * q : 4 * q + 4, :].bitcast(I32),
                     )
-            wh_raw.append(load_float_weight(wh, a, "wh_raw%d" % a))
-            if a == 0:
                 nc.sync.dma_start(head_list[:], offs2)
+                nc.sync.dma_start(bg_cols[:], bg.rearrange("(a p t) -> p a t", a=PASSES, t=PACK))
+            wh_raw.append(load_float_weight(wh, a, "wh_raw%d" % a))
         nc.sync.dma_start(wo_codes[:].bitcast(I32), wo_words.rearrange("a p c -> p a c").bitcast(I32))
         for q in range(4):
             nc.sync.dma_start(
@@ -102,32 +101,33 @@ def tile_list_compound_gate_features_kernel(
         with nc.allow_non_contiguous_dma(reason="bias, one value a partition"):
             nc.sync.dma_start(bo_cols[:], bo.rearrange("(n p) -> p n", p=P))
 
-        def gather(name, offsets):
-            words = keep.tile([P, S], U16, name=name + "_words", align_bytes=64)
-            scales = keep.tile([P, S], U8, name=name + "_scales", align_bytes=64)
-            return words, scales
-
-        v_mod = gather("v_mod", mod_list)
-        v_head = gather("v_head", head_list)
+        v_mod = (
+            keep.tile([P, S], U16, name="v_mod_words", align_bytes=64),
+            keep.tile([P, S], U8, name="v_mod_scales", align_bytes=64),
+        )
         nc.vector.tensor_copy(v_mod[0][:], table_words[:].indirect(mod_list[:]))
         nc.vector.tensor_copy(v_mod[1][:], table_scales[:].indirect(mod_list[:]))
-        nc.vector.tensor_copy(v_head[0][:], table_words[:].indirect(head_list[:]))
-        nc.vector.tensor_copy(v_head[1][:], table_scales[:].indirect(head_list[:]))
 
         def operand(name):
             codes = keep.tile([P, BANK], U32, name=name + "_codes", align_bytes=64)
             scales = keep.tile([P, BANK], U8, name=name + "_plane", align_bytes=64)
             return codes, scales
 
-        def round_weight(raw, sign, name):
-            rounded = keep.tile([P, BANK * PACK], BF16, name=name, align_bytes=64)
-            nc.scalar.activation(
-                rounded[:].rearrange("p (t m j) -> p m t j", t=PACK, j=PACK),
-                raw[:].rearrange("p j (m t) -> p m t j", t=PACK),
-                ACT.Copy,
-                scale=sign,
-            )
-            return rounded
+        def quantise_weight(raw, sign, name):
+            halves = []
+            for u in range(0, PACK, 2):
+                rounded = keep.tile([P, 2 * P * PACK], BF16, name="%s_round%d" % (name, u), tag="%s_round%d" % (name, u), align_bytes=64)
+                nc.scalar.activation(
+                    rounded[:].rearrange("p (t m j) -> p m j t", t=2, j=PACK),
+                    raw[:].rearrange("p j (m t) -> p m j t", t=PACK)[:, :, :, u : u + 2],
+                    ACT.Copy,
+                    scale=sign,
+                )
+                codes = keep.tile([P, 2 * P], U32, name="%s_codes%d" % (name, u), align_bytes=64)
+                plane = keep.tile([P, 2 * P], U8, name="%s_plane%d" % (name, u), align_bytes=64)
+                quantise(rounded[:], (codes, plane), slice(0, 2 * P))
+                halves.extend((codes[:, P * e : P * (e + 1)], plane[:, P * e : P * (e + 1)]) for e in range(2))
+            return halves
 
         def quantise(rounded, dst, cols):
             codes, scales = dst
@@ -147,24 +147,13 @@ def tile_list_compound_gate_features_kernel(
                 scales[:].rearrange("p (t m) -> p t m", t=PACK),
                 wm_raw_scales[:, BANK * a : BANK * (a + 1)].rearrange("p (m t) -> p t m", t=PACK),
             )
-            return codes, scales
-
-        def prepare(a):
-            whole = slice(0, BANK)
-            g_op, h_op = operand("wg%d" % a), operand("wh%d" % a)
-            g_round = round_weight(wg_raw[a], 1.0, "wg_round%d" % a)
-            h_round = round_weight(wh_raw[a], -1.0, "wh_round%d" % a)
-            quantise(g_round[:], g_op, whole)
-            m_op = reorder_wm(a)
-            quantise(h_round[:], h_op, whole)
-            return g_op, m_op, h_op
+            return [(codes[:, P * t : P * (t + 1)], scales[:, P * t : P * (t + 1)]) for t in range(PACK)]
 
         def product(dst, weight, t, v, cols, start=True, stop=True):
-            rows = slice(P * t, P * (t + 1))
             nc.tensor.matmul_mx(
                 out=dst,
-                lhsT=weight[0][:, rows].bitcast(FP8X4),
-                lhsT_scale=weight[1][:, rows],
+                lhsT=weight[t][0].bitcast(FP8X4),
+                lhsT_scale=weight[t][1],
                 rhs=v[0][:, cols].bitcast(FP4X4),
                 rhs_scale=v[1][:, cols],
                 start=start,
@@ -174,7 +163,10 @@ def tile_list_compound_gate_features_kernel(
         def gate_of(weights, a, t, cols):
             pre = psum.tile([P, BANK], F32, name="pre", tag="pre")
             product(pre[:], weights[0], t, v_mod, cols)
-            gate = work.tile([P, BANK], F32, name="gate", tag="gate", bufs=6)
+            if (a, t, cols.start) in HELD:
+                gate = keep.tile([P, BANK], F32, name="gate_held", tag=HELD[(a, t, cols.start)], align_bytes=64)
+            else:
+                gate = work.tile([P, BANK], F32, name="gate", tag="gate", bufs=8)
             nc.scalar.activation(gate[:], pre[:], ACT.Sigmoid, bias=bg_cols[:, a, t : t + 1])
             return gate
 
@@ -182,7 +174,7 @@ def tile_list_compound_gate_features_kernel(
             nc.vector.scalar_tensor_tensor(dst, gate[:], 1.0, bank[:], ALU.subtract, ALU.mult)
 
         def difference(weights, t, cols):
-            bank = psum.tile([P, BANK], F32, name="diff", tag="head")
+            bank = psum.tile([P, BANK], F32, name="diff", tag="prod", bufs=6)
             product(bank[:], weights[1], t, v_mod, cols, stop=False)
             product(bank[:], weights[2], t, v_head, cols, start=False)
             return bank
@@ -190,14 +182,14 @@ def tile_list_compound_gate_features_kernel(
         def terms(weights, a, c, t, first, second):
             cols = slice(BANK * c, BANK * (c + 1))
             gate = gate_of(weights, a, t, cols)
-            mod = psum.tile([P, BANK], F32, name="mod", tag="mod")
+            mod = psum.tile([P, BANK], F32, name="mod", tag="prod", bufs=6)
             product(mod[:], weights[1], t, v_mod, cols)
             if (a, c, t) in REPEATED:
                 diff = difference(weights, t, cols)
                 nc.scalar.copy(first[:, t, :], mod[:])
                 gate_less_one_times(second[:, t, :], gate, diff)
             else:
-                less_head = psum.tile([P, BANK], F32, name="less_head", tag="head")
+                less_head = psum.tile([P, BANK], F32, name="less_head", tag="prod", bufs=6)
                 product(less_head[:], weights[2], t, v_head, cols)
                 nc.vector.tensor_tensor(first[:, t, :], gate[:], mod[:], ALU.mult)
                 gate_less_one_times(second[:, t, :], gate, less_head)
@@ -221,72 +213,92 @@ def tile_list_compound_gate_features_kernel(
                 )
 
         out_rows = out.rearrange("(n p) j -> p n j", p=P)
-        h_ops = {}
 
         def group_terms(weights, a, c):
-            first = work.tile([P, PACK, BANK], F32, name="first", tag="first")
-            second = work.tile([P, PACK, BANK], F32, name="second", tag="second")
+            first = work.tile([P, PACK, BANK], F32, name="first", tag="first", bufs=3)
+            second = work.tile([P, PACK, BANK], F32, name="second", tag="second", bufs=3)
             for t in range(PACK):
                 terms(weights, a, c, t, first, second)
             return first, second
 
-        def group_sum(a, c, first, second):
-            h_round = work.tile([P, BANK * PACK], BF16, name="h_round", tag="h_round", align_bytes=64)
-            for b in range(BANK // PIECE):
-                js = slice(PIECE * b, PIECE * (b + 1))
-                engine = nc.gpsimd if (a, c, b) in ADD_ON_GPSIMD else nc.vector
-                add_and_round(
-                    engine, h_round[:, PACK * PIECE * b : PACK * PIECE * (b + 1)], first[:, :, js], second[:, :, js]
-                )
-            return h_round
-
-        def group_quantise(a, c, h_round):
-            h_ops[(a, c)] = operand("h%d%d" % (a, c))
-            quantise(h_round[:], h_ops[(a, c)], slice(0, BANK))
-
-        def features_whole(c):
+        def features_whole(c, h_ops):
             for n in range(N // P):
-                acc = psum.tile([P, BANK], F32, name="acc", tag="acc")
-                last_product(acc[:], n, [h_ops[(a, c)] for a in range(PASSES)], slice(0, BANK))
+                acc = psum.tile([P, BANK], F32, name="acc", tag="prod", bufs=6)
+                last_product(acc[:], n, h_ops, slice(0, BANK))
                 res = work.tile([P, BANK], F32, name="res", tag="res", bufs=4)
                 nc.scalar.activation(res[:], acc[:], ACT.Identity, bias=bo_cols[:, n : n + 1])
                 nc.sync.dma_start(out_rows[:, n, BANK * c : BANK * (c + 1)], res[:])
 
-        w0 = prepare(0)
-        t00 = group_terms(w0, 0, 0)
-        w1 = prepare(1)
-        t10 = group_terms(w1, 1, 0)
-        group_quantise(0, 0, group_sum(0, 0, *t00))
-        t01 = group_terms(w0, 0, 1)
-        group_quantise(1, 0, group_sum(1, 0, *t10))
+        pieces = BANK // PIECE
 
-        a, c = PASSES - 1, CHUNKS - 1
-        cols = slice(BANK * c, BANK * (c + 1))
-        scaled = keep.tile([P, PACK, BANK], F32, name="scaled")
+        def piece_cols(b, first=0):
+            return slice(first + PIECE * b, first + PIECE * (b + 1))
+
+        def words_of(b):
+            return slice(PACK * PIECE * b, PACK * PIECE * (b + 1))
+
+        def h_operand(name, rounded, width):
+            codes = keep.tile([P, width], U32, name=name + "_codes", tag=name + "_codes", align_bytes=64)
+            plane = keep.tile([P, width], U8, name=name + "_plane", align_bytes=64)
+            quantise(rounded, (codes, plane), slice(0, width))
+            return codes, plane
+
+        wm0 = reorder_wm(0)
+        wg0 = quantise_weight(wg_raw[0], 1.0, "wg0")
+        v_head = (
+            keep.tile([P, S], U16, name="v_head_words", tag="wg0_round2", align_bytes=64),
+            keep.tile([P, S], U8, name="v_head_scales", tag="wg_raw0", align_bytes=64),
+        )
+        nc.vector.tensor_copy(v_head[0][:], table_words[:].indirect(head_list[:]))
+        nc.vector.tensor_copy(v_head[1][:], table_scales[:].indirect(head_list[:]))
+        w0 = (wg0, wm0, quantise_weight(wh_raw[0], -1.0, "wh0"))
+        w1 = (quantise_weight(wg_raw[1], 1.0, "wg1"), reorder_wm(1), quantise_weight(wh_raw[1], -1.0, "wh1"))
+
+        h_early = keep.tile([P, PASSES, BANK * PACK], BF16, name="h_early", tag="wh1_round2", align_bytes=64)
+        first, second = group_terms(w0, 0, 0)
+        for b in range(pieces):
+            add_and_round(nc.gpsimd, h_early[:, 0, words_of(b)], first[:, :, piece_cols(b)], second[:, :, piece_cols(b)])
+
+        scaled = work.tile([P, PACK, BANK], F32, name="scaled", tag="second", bufs=3)
         for t in range(PACK):
-            gate = gate_of(w1, a, t, cols)
-            gate_less_one_times(scaled[:, t, :], gate, difference(w1, t, cols))
-        features_whole(0)
-
-        def tail_sum(b):
-            js = slice(PIECE * b, PIECE * (b + 1))
-            h_piece = keep.tile([P, PASSES, PACK * PIECE], BF16, name="h_piece%d" % b, align_bytes=64)
-            engine = nc.gpsimd if (0, c, b) in ADD_ON_GPSIMD else nc.vector
-            add_and_round(engine, h_piece[:, 0, :], t01[0][:, :, js], t01[1][:, :, js])
-            mod = psum.tile([P, PACK, PIECE], F32, name="mod_piece", tag="mod")
+            gate = gate_of(w1, 1, t, slice(0, BANK))
+            gate_less_one_times(scaled[:, t, :], gate, difference(w1, t, slice(0, BANK)))
+        for b in range(pieces):
+            mod = psum.tile([P, PACK, PIECE], F32, name="mod_piece", tag="prod", bufs=6)
             for t in range(PACK):
-                product(mod[:, t, :], w1[1], t, v_mod, slice(BANK * c + PIECE * b, BANK * c + PIECE * (b + 1)))
-            add_and_round(nc.vector, h_piece[:, 1, :], scaled[:, :, js], mod[:])
-            return h_piece
+                product(mod[:, t, :], w1[1], t, v_mod, piece_cols(b))
+            add_and_round(nc.vector, h_early[:, 1, words_of(b)], scaled[:, :, piece_cols(b)], mod[:])
 
-        def tail_features(b, h_piece):
-            codes = keep.tile([P, PASSES * PIECE], U32, name="h_tail_codes%d" % b, align_bytes=64)
-            scales = keep.tile([P, PASSES * PIECE], U8, name="h_tail_plane%d" % b, align_bytes=64)
-            quantise(h_piece[:].rearrange("p a x -> p (a x)"), (codes, scales), slice(0, PASSES * PIECE))
-            acc = psum.tile([P, N // P, PIECE], F32, name="acc_piece", tag="acc")
-            halves = [slice(PIECE * k, PIECE * (k + 1)) for k in range(PASSES)]
+        first = work.tile([P, PACK, BANK], F32, name="first", tag="first", bufs=3)
+        second = work.tile([P, PACK, BANK], F32, name="second", tag="second", bufs=3)
+        for t in range(1 + 1):
+            terms(w0, 0, 1, t, first, second)
+        early = h_operand("h_early", h_early[:].rearrange("p a x -> p (a x)"), PASSES * BANK)
+        for t in range(1 + 1, PACK):
+            terms(w0, 0, 1, t, first, second)
+        late = [(first, second), group_terms(w1, 1, 1)]
+        features_whole(0, [(early[0][:, BANK * a : BANK * (a + 1)], early[1][:, BANK * a : BANK * (a + 1)]) for a in range(PASSES)])
+
+        h_tail = [
+            keep.tile([P, 2, PASSES, PACK * PIECE], BF16, name="h_tail%d" % b, tag="h_tail%d" % b, align_bytes=64)
+            for b in range(0, pieces, 2)
+        ]
+
+        def tail_sum(a, b):
+            engine = nc.gpsimd if a == 0 and b < TAIL_GPSIMD else nc.vector
+            add_and_round(engine, h_tail[b // 2][:, b % 2, a, :], late[a][0][:, :, piece_cols(b)], late[a][1][:, :, piece_cols(b)])
+
+        def tail_quantise(start, count):
+            rounded = h_tail[start // 2][:, start % 2 : start % 2 + count].rearrange("p b a x -> p (b a x)")
+            codes, plane = h_operand("h_late%d" % start, rounded, count * PASSES * PIECE)
+            for i in range(count):
+                tail_features(start + i, codes, plane, i * PASSES * PIECE)
+
+        def tail_features(b, codes, plane, at):
+            acc = psum.tile([P, N // P, PIECE], F32, name="acc_piece", tag="prod", bufs=6)
+            halves = [slice(at + PIECE * a, at + PIECE * (a + 1)) for a in range(PASSES)]
             for n in range(N // P):
-                last_product(acc[:, n, :], n, [(codes[:, x], scales[:, x]) for x in halves], slice(0, PIECE))
+                last_product(acc[:, n, :], n, [(codes[:, x], plane[:, x]) for x in halves], slice(0, PIECE))
             res = keep.tile([P, N // P, PIECE], F32, name="res_piece%d" % b)
             if b in TAIL_ON_VECTOR:
                 nc.vector.tensor_tensor(
@@ -295,12 +307,16 @@ def tile_list_compound_gate_features_kernel(
             else:
                 for n in range(N // P):
                     nc.scalar.activation(res[:, n, :], acc[:, n, :], ACT.Identity, bias=bo_cols[:, n : n + 1])
-            nc.sync.dma_start(out_rows[:, :, BANK * c + PIECE * b : BANK * c + PIECE * (b + 1)], res[:])
+            nc.sync.dma_start(out_rows[:, :, piece_cols(b, BANK)], res[:])
 
-        pending = None
-        for b in range(BANK // PIECE):
-            piece = tail_sum(b)
-            if pending is not None:
-                tail_features(b - 1, pending)
-            pending = piece
-        tail_features(BANK // PIECE - 1, pending)
+        tail_sum(0, 0)
+        tail_sum(0, 1)
+        tail_sum(1, 0)
+        tail_sum(1, 1)
+        tail_sum(0, 2)
+        tail_quantise(0, 2)
+        tail_sum(1, 2)
+        tail_sum(0, 3)
+        tail_quantise(2, 1)
+        tail_sum(1, 3)
+        tail_quantise(3, 1)

@@ -3,7 +3,7 @@ from contextlib import ExitStack
 import concourse.mybir as mybir
 
 K, H, N, T, S = 512, 1024, 512, 4096, 1024
-FLOPS = 2 * K * H * S * 3 + 2 * H * N * S
+FLOPS = 3 * 2 * K * H * S + 2 * H * N * S
 
 F32 = mybir.dt.float32
 BF16 = mybir.dt.bfloat16
@@ -18,15 +18,15 @@ ALU = mybir.AluOpType
 
 P = 128
 PACK = 4
+QUADRANTS = 4
 BANK = 512
-PIECE = 128
+PIECE = BANK // PACK
+PIECES = BANK // PIECE
 PASSES = H // (P * PACK)
-CHUNKS = S // BANK
-REPEATED = frozenset([(0, 0, 3), (1, 1, 3)])
-TAIL_GPSIMD = 2
-TAIL_ON_VECTOR = (3,)
-HELD = {(0, 1, BANK): "h_early_codes", (1, 3, BANK): "h_tail2"}
-WARM = True
+OUT_TILES = N // P
+GATE_BANKS = 2
+SUM_BANKS = 6
+GATE_TILES = 8
 
 
 def tile_list_compound_gate_features_kernel(
@@ -36,287 +36,251 @@ def tile_list_compound_gate_features_kernel(
     with ExitStack() as ctx:
         lists = ctx.enter_context(tc.tile_pool(name="lists", bufs=1))
         keep = ctx.enter_context(tc.tile_pool(name="keep", bufs=1))
-        work = ctx.enter_context(tc.tile_pool(name="work", bufs=2))
-        psum = ctx.enter_context(tc.psum_pool(name="psum", bufs=2))
+        work = ctx.enter_context(tc.tile_pool(name="work", bufs=3))
+        psum = ctx.enter_context(tc.psum_pool(name="psum", bufs=SUM_BANKS))
 
         mod_list = lists.tile([P, S // 16], U16, name="mod_list")
         head_list = lists.tile([P, S // 16], U16, name="head_list")
-
         table_words = keep.tile([P, T], U16, name="table_words", align_bytes=64)
-        table_scales = keep.tile([P, T], U8, name="table_scales", align_bytes=64)
-        wm_raw_scales = keep.tile([P, H], U8, name="wm_raw_scales", align_bytes=64)
+        table_plane = keep.tile([P, T], U8, name="table_plane", align_bytes=64)
+        wm_loaded_words = keep.tile([P, H], I32, name="wm_loaded_words")
+        wm_loaded_plane = keep.tile([P, H], U8, name="wm_loaded_plane", align_bytes=64)
         wo_codes = keep.tile([P, PASSES, 2 * N], U8, name="wo_codes", align_bytes=64)
         wo_plane = keep.tile([P, PASSES, N], U8, name="wo_plane", align_bytes=64)
         bg_cols = keep.tile([P, PASSES, PACK], F32, name="bg_cols")
-        bo_cols = keep.tile([P, N // P], F32, name="bo_cols")
+        bo_cols = keep.tile([P, OUT_TILES], F32, name="bo_cols")
 
-        nc.vector.memset(table_scales[:].bitcast(I32), 0)
-        nc.gpsimd.memset(wm_raw_scales[:].bitcast(I32), 0)
+        nc.vector.memset(table_plane[:].bitcast(I32), 0)
+        nc.gpsimd.memset(wm_loaded_plane[:].bitcast(I32), 0)
         nc.gpsimd.memset(wo_plane[:].rearrange("p a c -> p (a c)").bitcast(I32), 0)
-        if WARM:
-            warm_in = keep.tile([P, 1], F32, name="warm_in")
-            warm_out = keep.tile([P, 1], F32, name="warm_out")
-            nc.gpsimd.memset(warm_in[:], 0.0)
-            nc.scalar.activation(warm_out[:], warm_in[:], ACT.Sigmoid)
+
+        def load_plane(plane, rows):
+            for q in range(QUADRANTS):
+                nc.sync.dma_start(plane[32 * q : 32 * q + 4].bitcast(I32), rows[4 * q : 4 * q + 4].bitcast(I32))
+
+        def load_float_weight(w, a, name):
+            raw = keep.tile([P, PACK, BANK], F32, name=name)
+            nc.sync.dma_start(raw[:], w[:, BANK * a : BANK * (a + 1)].rearrange("(p i) c -> p i c", i=PACK))
+            return raw
 
         nc.sync.dma_start(table_words[:].bitcast(I32), tab_words[0].bitcast(I32))
         nc.sync.dma_start(mod_list[:], offs)
-        for q in range(4):
-            nc.sync.dma_start(
-                table_scales[32 * q : 32 * q + 4, :].bitcast(I32), tab_scales[0, 4 * q : 4 * q + 4, :].bitcast(I32)
-            )
-
-        def load_float_weight(w, a, name):
-            raw = keep.tile([P, PACK, BANK], F32, name=name, tag=name, align_bytes=64)
-            nc.sync.dma_start(raw[:], w[:, BANK * a : BANK * (a + 1)].rearrange("(p j) c -> p j c", j=PACK))
-            return raw
-
-        def load_wm_words(a):
-            raw = keep.tile([P, BANK], I32, name="wm_raw%d" % a)
-            nc.sync.dma_start(
-                raw[:], wm_words[0].rearrange("p c i -> p (c i)")[:, 4 * BANK * a : 4 * BANK * (a + 1)].bitcast(I32)
-            )
-            return raw
-
-        wg_raw, wh_raw, wm_raw = [], [], []
-        for a in range(PASSES):
-            wg_raw.append(load_float_weight(wg, a, "wg_raw%d" % a))
-            wm_raw.append(load_wm_words(a))
-            if a == 0:
-                for q in range(4):
-                    nc.sync.dma_start(
-                        wm_raw_scales[32 * q : 32 * q + 4, :].bitcast(I32),
-                        wm_scales[0, 4 * q : 4 * q + 4, :].bitcast(I32),
-                    )
-                nc.sync.dma_start(head_list[:], offs2)
-                nc.sync.dma_start(bg_cols[:], bg.rearrange("(a p t) -> p a t", a=PASSES, t=PACK))
-            wh_raw.append(load_float_weight(wh, a, "wh_raw%d" % a))
+        nc.sync.dma_start(head_list[:], offs2)
+        load_plane(table_plane, tab_scales[0])
+        wg_raw = [load_float_weight(wg, 0, "wg_raw0")]
+        wh_raw = [load_float_weight(wh, 0, "wh_raw0")]
+        wg_raw.append(load_float_weight(wg, 1, "wg_raw1"))
+        nc.sync.dma_start(wm_loaded_words[:], wm_words[0].rearrange("p c i -> p (c i)").bitcast(I32))
+        load_plane(wm_loaded_plane, wm_scales[0])
+        nc.sync.dma_start(bg_cols[:], bg.rearrange("(a p t) -> p a t", a=PASSES, t=PACK))
+        wh_raw.append(load_float_weight(wh, 1, "wh_raw1"))
         nc.sync.dma_start(wo_codes[:].bitcast(I32), wo_words.rearrange("a p c -> p a c").bitcast(I32))
-        for q in range(4):
-            nc.sync.dma_start(
-                wo_plane[32 * q : 32 * q + 4, :, :].bitcast(I32),
-                wo_scales[:, 4 * q : 4 * q + 4, :].rearrange("a r c -> r a c").bitcast(I32),
-            )
-
-        with nc.allow_non_contiguous_dma(reason="bias, one value a partition"):
+        load_plane(wo_plane, wo_scales.rearrange("a q c -> q a c"))
+        with nc.allow_non_contiguous_dma(reason="bo lies one value a partition for each output tile"):
             nc.sync.dma_start(bo_cols[:], bo.rearrange("(n p) -> p n", p=P))
 
-        v_mod = (
-            keep.tile([P, S], U16, name="v_mod_words", align_bytes=64),
-            keep.tile([P, S], U8, name="v_mod_scales", align_bytes=64),
-        )
-        nc.vector.tensor_copy(v_mod[0][:], table_words[:].indirect(mod_list[:]))
-        nc.vector.tensor_copy(v_mod[1][:], table_scales[:].indirect(mod_list[:]))
+        def columns(operand, start, width):
+            return operand[0][:, start : start + width], operand[1][:, start : start + width]
 
-        def operand(name):
-            codes = keep.tile([P, BANK], U32, name=name + "_codes", align_bytes=64)
-            scales = keep.tile([P, BANK], U8, name=name + "_plane", align_bytes=64)
-            return codes, scales
+        def gather(name, table, offsets):
+            picked = keep.tile([P, S], table.dtype, name=name, align_bytes=64)
+            nc.vector.tensor_copy(picked[:], table.indirect(offsets[:]))
+            return picked[:]
 
-        def quantise_weight(raw, sign, name):
-            halves = []
-            for u in range(0, PACK, 2):
-                rounded = keep.tile([P, 2 * P * PACK], BF16, name="%s_round%d" % (name, u), tag="%s_round%d" % (name, u), align_bytes=64)
-                nc.scalar.activation(
-                    rounded[:].rearrange("p (t m j) -> p m j t", t=2, j=PACK),
-                    raw[:].rearrange("p j (m t) -> p m j t", t=PACK)[:, :, :, u : u + 2],
-                    ACT.Copy,
-                    scale=sign,
-                )
-                codes = keep.tile([P, 2 * P], U32, name="%s_codes%d" % (name, u), align_bytes=64)
-                plane = keep.tile([P, 2 * P], U8, name="%s_plane%d" % (name, u), align_bytes=64)
-                quantise(rounded[:], (codes, plane), slice(0, 2 * P))
-                halves.extend((codes[:, P * e : P * (e + 1)], plane[:, P * e : P * (e + 1)]) for e in range(2))
-            return halves
+        def quantise(name, rounded):
+            width = rounded.shape[1] // PACK
+            words = keep.tile([P, width], U32, name=name + "_words", tag=name + "_words", align_bytes=64)
+            plane = keep.tile([P, width], U8, name=name + "_plane", align_bytes=64)
+            nc.vector.quantize_mx(out=words[:].bitcast(FP8X4), scales=plane[:], in_=rounded)
+            return words[:], plane[:]
 
-        def quantise(rounded, dst, cols):
-            codes, scales = dst
-            nc.vector.quantize_mx(
-                out=codes[:, cols].bitcast(FP8X4),
-                scales=scales[:, cols],
-                in_=rounded,
-            )
+        def quantise_weight(name, raw, sign):
+            rounded = keep.tile([P, BANK * PACK], BF16, name=name + "_round", tag=name + "_round", align_bytes=64)
+            dst = rounded[:].rearrange("p (t m i) -> p m i t", t=PACK, i=PACK)
+            src = raw[:].rearrange("p i (m t) -> p m i t", t=PACK)
+            for t in range(0, PACK, 2):
+                nc.scalar.activation(dst[:, :, :, t : t + 2], src[:, :, :, t : t + 2], ACT.Copy, scale=sign)
+            return quantise(name, rounded[:])
 
-        def reorder_wm(a):
-            codes, scales = operand("wm%d" % a)
+        def reorder_wm():
+            words = keep.tile([P, H], U32, name="wm_words", align_bytes=64)
+            plane = keep.tile([P, H], U8, name="wm_plane", align_bytes=64)
             nc.vector.tensor_copy(
-                codes[:].bitcast(I32).rearrange("p (t m e) -> p m t e", t=PACK, e=2),
-                wm_raw[a][:].rearrange("p (m e t) -> p m t e", t=PACK, e=2),
+                words[:].bitcast(I32).rearrange("p (a t m e) -> p a m t e", a=PASSES, t=PACK, e=2),
+                wm_loaded_words[:].rearrange("p (a m e t) -> p a m t e", a=PASSES, t=PACK, e=2),
             )
             nc.vector.tensor_copy(
-                scales[:].rearrange("p (t m) -> p t m", t=PACK),
-                wm_raw_scales[:, BANK * a : BANK * (a + 1)].rearrange("p (m t) -> p t m", t=PACK),
+                plane[:].rearrange("p (a t m) -> p a t m", a=PASSES, t=PACK),
+                wm_loaded_plane[:].rearrange("p (a m t) -> p a t m", a=PASSES, t=PACK),
             )
-            return [(codes[:, P * t : P * (t + 1)], scales[:, P * t : P * (t + 1)]) for t in range(PACK)]
+            return words[:], plane[:]
 
-        def product(dst, weight, t, v, cols, start=True, stop=True):
+        mod_words = gather("mod_words", table_words[:], mod_list)
+        head_words = gather("head_words", table_words[:], head_list)
+        v_mod = mod_words, gather("mod_plane", table_plane[:], mod_list)
+        v_head = head_words, gather("head_plane", table_plane[:], head_list)
+        wg_ops = [quantise_weight("wg0", wg_raw[0], 1.0)]
+        less_wh_ops = [quantise_weight("wh0", wh_raw[0], -1.0)]
+        wm_all = reorder_wm()
+        wm_ops = [columns(wm_all, BANK * a, BANK) for a in range(PASSES)]
+        wg_ops.append(quantise_weight("wg1", wg_raw[1], 1.0))
+        less_wh_ops.append(quantise_weight("wh1", wh_raw[1], -1.0))
+
+        def product(dst, weight, t, v, start_col, width, start=True, stop=True):
+            lhs, rhs = columns(weight, P * t, P), columns(v, start_col, width)
             nc.tensor.matmul_mx(
                 out=dst,
-                lhsT=weight[t][0].bitcast(FP8X4),
-                lhsT_scale=weight[t][1],
-                rhs=v[0][:, cols].bitcast(FP4X4),
-                rhs_scale=v[1][:, cols],
+                lhsT=lhs[0].bitcast(FP8X4),
+                lhsT_scale=lhs[1],
+                rhs=rhs[0].bitcast(FP4X4),
+                rhs_scale=rhs[1],
                 start=start,
                 stop=stop,
             )
 
-        def gate_of(weights, a, t, cols):
-            pre = psum.tile([P, BANK], F32, name="pre", tag="pre")
-            product(pre[:], weights[0], t, v_mod, cols)
-            if (a, t, cols.start) in HELD:
-                gate = keep.tile([P, BANK], F32, name="gate_held", tag=HELD[(a, t, cols.start)], align_bytes=64)
+        def sum_bank(shape, name):
+            return psum.tile(shape, F32, name=name, tag="sums")
+
+        def gate_of(a, c, t, lend_to):
+            pre = psum.tile([P, BANK], F32, name="pre", tag="pre", bufs=GATE_BANKS)
+            product(pre[:], wg_ops[a], t, v_mod, BANK * c, BANK)
+            if lend_to:
+                gate = keep.tile([P, BANK], F32, name="lent_gate", tag=lend_to, align_bytes=64)
             else:
-                gate = work.tile([P, BANK], F32, name="gate", tag="gate", bufs=8)
+                gate = work.tile([P, BANK], F32, name="gate", tag="gate", bufs=GATE_TILES)
             nc.scalar.activation(gate[:], pre[:], ACT.Sigmoid, bias=bg_cols[:, a, t : t + 1])
             return gate
 
         def gate_less_one_times(dst, gate, bank):
             nc.vector.scalar_tensor_tensor(dst, gate[:], 1.0, bank[:], ALU.subtract, ALU.mult)
 
-        def difference(weights, t, cols):
-            bank = psum.tile([P, BANK], F32, name="diff", tag="prod", bufs=6)
-            product(bank[:], weights[1], t, v_mod, cols, stop=False)
-            product(bank[:], weights[2], t, v_head, cols, start=False)
+        def mod_less_head(a, c, t):
+            bank = sum_bank([P, BANK], "mod_less_head")
+            product(bank[:], wm_ops[a], t, v_mod, BANK * c, BANK, stop=False)
+            product(bank[:], less_wh_ops[a], t, v_head, BANK * c, BANK, start=False)
             return bank
 
-        def terms(weights, a, c, t, first, second):
-            cols = slice(BANK * c, BANK * (c + 1))
-            gate = gate_of(weights, a, t, cols)
-            mod = psum.tile([P, BANK], F32, name="mod", tag="prod", bufs=6)
-            product(mod[:], weights[1], t, v_mod, cols)
-            if (a, c, t) in REPEATED:
-                diff = difference(weights, t, cols)
-                nc.scalar.copy(first[:, t, :], mod[:])
-                gate_less_one_times(second[:, t, :], gate, diff)
-            else:
-                less_head = psum.tile([P, BANK], F32, name="less_head", tag="prod", bufs=6)
-                product(less_head[:], weights[2], t, v_head, cols)
-                nc.vector.tensor_tensor(first[:, t, :], gate[:], mod[:], ALU.mult)
-                gate_less_one_times(second[:, t, :], gate, less_head)
+        def term_tiles():
+            return (
+                work.tile([P, PACK, BANK], F32, name="first", tag="first"),
+                work.tile([P, PACK, BANK], F32, name="second", tag="second"),
+            )
 
-        def pairs(ap):
-            return ap.rearrange("p t (c i) -> p c t i", i=2)
+        def unit_terms(a, c, t, terms, repeat=False, lend_to=None):
+            gate = gate_of(a, c, t, lend_to)
+            mod = sum_bank([P, BANK], "mod")
+            product(mod[:], wm_ops[a], t, v_mod, BANK * c, BANK)
+            if repeat:
+                other = mod_less_head(a, c, t)
+                nc.scalar.copy(terms[0][:, t, :], mod[:])
+            else:
+                other = sum_bank([P, BANK], "less_head")
+                product(other[:], less_wh_ops[a], t, v_head, BANK * c, BANK)
+                nc.vector.tensor_tensor(terms[0][:, t, :], gate[:], mod[:], ALU.mult)
+            gate_less_one_times(terms[1][:, t, :], gate, other)
+
+        def piece_of(term, b):
+            return term[:, :, PIECE * b : PIECE * (b + 1)]
 
         def add_and_round(engine, dst, first, second):
-            engine.tensor_tensor(dst.rearrange("p (c i t) -> p c t i", i=2, t=PACK), pairs(first), pairs(second), ALU.add)
-
-        def last_product(dst, n, h_ops, cols):
-            for a in range(PASSES):
-                nc.tensor.matmul_mx(
-                    out=dst,
-                    lhsT=wo_codes[:, a, 2 * P * n : 2 * P * (n + 1)].bitcast(FP4X4),
-                    lhsT_scale=wo_plane[:, a, P * n : P * (n + 1)],
-                    rhs=h_ops[a][0][:, cols].bitcast(FP8X4),
-                    rhs_scale=h_ops[a][1][:, cols],
-                    start=(a == 0),
-                    stop=(a == PASSES - 1),
-                )
+            engine.tensor_tensor(
+                dst.rearrange("p (c e t) -> p c t e", e=2, t=PACK),
+                first.rearrange("p t (c e) -> p c t e", e=2),
+                second.rearrange("p t (c e) -> p c t e", e=2),
+                ALU.add,
+            )
 
         out_rows = out.rearrange("(n p) j -> p n j", p=P)
 
-        def group_terms(weights, a, c):
-            first = work.tile([P, PACK, BANK], F32, name="first", tag="first", bufs=3)
-            second = work.tile([P, PACK, BANK], F32, name="second", tag="second", bufs=3)
-            for t in range(PACK):
-                terms(weights, a, c, t, first, second)
-            return first, second
+        def last_pass(dst, n, a, h_op, start, stop):
+            nc.tensor.matmul_mx(
+                out=dst,
+                lhsT=wo_codes[:, a, 2 * P * n : 2 * P * (n + 1)].bitcast(FP4X4),
+                lhsT_scale=wo_plane[:, a, P * n : P * (n + 1)],
+                rhs=h_op[0].bitcast(FP8X4),
+                rhs_scale=h_op[1],
+                start=start,
+                stop=stop,
+            )
 
-        def features_whole(c, h_ops):
-            for n in range(N // P):
-                acc = psum.tile([P, BANK], F32, name="acc", tag="prod", bufs=6)
-                last_product(acc[:], n, h_ops, slice(0, BANK))
-                res = work.tile([P, BANK], F32, name="res", tag="res", bufs=4)
-                nc.scalar.activation(res[:], acc[:], ACT.Identity, bias=bo_cols[:, n : n + 1])
-                nc.sync.dma_start(out_rows[:, n, BANK * c : BANK * (c + 1)], res[:])
+        def add_bo_on_scalar(dst, acc, n):
+            nc.scalar.activation(dst, acc, ACT.Identity, bias=bo_cols[:, n : n + 1])
 
-        pieces = BANK // PIECE
-
-        def piece_cols(b, first=0):
-            return slice(first + PIECE * b, first + PIECE * (b + 1))
-
-        def words_of(b):
-            return slice(PACK * PIECE * b, PACK * PIECE * (b + 1))
-
-        def h_operand(name, rounded, width):
-            codes = keep.tile([P, width], U32, name=name + "_codes", tag=name + "_codes", align_bytes=64)
-            plane = keep.tile([P, width], U8, name=name + "_plane", align_bytes=64)
-            quantise(rounded, (codes, plane), slice(0, width))
-            return codes, plane
-
-        wm0 = reorder_wm(0)
-        wg0 = quantise_weight(wg_raw[0], 1.0, "wg0")
-        v_head = (
-            keep.tile([P, S], U16, name="v_head_words", tag="wg0_round2", align_bytes=64),
-            keep.tile([P, S], U8, name="v_head_scales", tag="wg_raw0", align_bytes=64),
-        )
-        nc.vector.tensor_copy(v_head[0][:], table_words[:].indirect(head_list[:]))
-        nc.vector.tensor_copy(v_head[1][:], table_scales[:].indirect(head_list[:]))
-        w0 = (wg0, wm0, quantise_weight(wh_raw[0], -1.0, "wh0"))
-        w1 = (quantise_weight(wg_raw[1], 1.0, "wg1"), reorder_wm(1), quantise_weight(wh_raw[1], -1.0, "wh1"))
-
-        h_early = keep.tile([P, PASSES, BANK * PACK], BF16, name="h_early", tag="wh1_round2", align_bytes=64)
-        first, second = group_terms(w0, 0, 0)
-        for b in range(pieces):
-            add_and_round(nc.gpsimd, h_early[:, 0, words_of(b)], first[:, :, piece_cols(b)], second[:, :, piece_cols(b)])
-
-        scaled = work.tile([P, PACK, BANK], F32, name="scaled", tag="second", bufs=3)
+        h_early = keep.tile([P, PASSES, PIECES, PACK * PIECE], BF16, name="h_early", tag="wh1_round", align_bytes=64)
+        terms = term_tiles()
         for t in range(PACK):
-            gate = gate_of(w1, 1, t, slice(0, BANK))
-            gate_less_one_times(scaled[:, t, :], gate, difference(w1, t, slice(0, BANK)))
-        for b in range(pieces):
-            mod = psum.tile([P, PACK, PIECE], F32, name="mod_piece", tag="prod", bufs=6)
+            unit_terms(0, 0, t, terms, repeat=(t == PACK - 1))
+        for b in range(PIECES):
+            add_and_round(nc.gpsimd, h_early[:, 0, b, :], piece_of(terms[0], b), piece_of(terms[1], b))
+
+        scaled = work.tile([P, PACK, BANK], F32, name="scaled", tag="second")
+        for t in range(PACK):
+            gate_less_one_times(scaled[:, t, :], gate_of(1, 0, t, None), mod_less_head(1, 0, t))
+        for b in range(PIECES):
+            mod = sum_bank([P, PACK, PIECE], "mod_piece")
             for t in range(PACK):
-                product(mod[:, t, :], w1[1], t, v_mod, piece_cols(b))
-            add_and_round(nc.vector, h_early[:, 1, words_of(b)], scaled[:, :, piece_cols(b)], mod[:])
+                product(mod[:, t, :], wm_ops[1], t, v_mod, PIECE * b, PIECE)
+            add_and_round(nc.vector, h_early[:, 1, b, :], piece_of(scaled, b), mod[:])
 
-        first = work.tile([P, PACK, BANK], F32, name="first", tag="first", bufs=3)
-        second = work.tile([P, PACK, BANK], F32, name="second", tag="second", bufs=3)
-        for t in range(1 + 1):
-            terms(w0, 0, 1, t, first, second)
-        early = h_operand("h_early", h_early[:].rearrange("p a x -> p (a x)"), PASSES * BANK)
-        for t in range(1 + 1, PACK):
-            terms(w0, 0, 1, t, first, second)
-        late = [(first, second), group_terms(w1, 1, 1)]
-        features_whole(0, [(early[0][:, BANK * a : BANK * (a + 1)], early[1][:, BANK * a : BANK * (a + 1)]) for a in range(PASSES)])
+        late = [term_tiles(), term_tiles()]
+        half = PACK // 2
+        for t in range(half):
+            unit_terms(0, 1, t, late[0], lend_to="h_early_words" if t == half - 1 else None)
+        early = quantise("h_early", h_early[:].rearrange("p a b x -> p (a b x)"))
+        for t in range(half, PACK):
+            unit_terms(0, 1, t, late[0], repeat=(t == PACK - 1))
+        for t in range(PACK):
+            unit_terms(1, 1, t, late[1], lend_to="h_late0_1" if t == PACK - 1 else None)
 
-        h_tail = [
-            keep.tile([P, 2, PASSES, PACK * PIECE], BF16, name="h_tail%d" % b, tag="h_tail%d" % b, align_bytes=64)
-            for b in range(0, pieces, 2)
+        for n in range(OUT_TILES):
+            acc = sum_bank([P, BANK], "acc")
+            for a in range(PASSES):
+                last_pass(acc[:], n, a, columns(early, BANK * a, BANK), a == 0, a == PASSES - 1)
+            res = work.tile([P, BANK], F32, name="res", tag="res", bufs=OUT_TILES)
+            add_bo_on_scalar(res[:], acc[:], n)
+            nc.sync.dma_start(out_rows[:, n, 0:BANK], res[:])
+
+        banks = [sum_bank([P, OUT_TILES, PIECE], "acc_piece%d" % b) for b in range(PIECES)]
+
+        def late_sum(engine, a, b, dst):
+            add_and_round(engine, dst, piece_of(late[a][0], b), piece_of(late[a][1], b))
+
+        def piece_pass(a, b, h_op):
+            for n in range(OUT_TILES):
+                last_pass(banks[b][:, n, :], n, a, h_op, a == 0 and n == 0, a == PASSES - 1 and n == OUT_TILES - 1)
+
+        pairs = [
+            keep.tile([P, 2, PACK * PIECE], BF16, name="h_late0_%d" % i, tag="h_late0_%d" % i, align_bytes=64)
+            for i in range(PIECES // 2)
         ]
+        singles = [keep.tile([P, PACK * PIECE], BF16, name="h_late1_%d" % b, align_bytes=64) for b in range(PIECES)]
 
-        def tail_sum(a, b):
-            engine = nc.gpsimd if a == 0 and b < TAIL_GPSIMD else nc.vector
-            add_and_round(engine, h_tail[b // 2][:, b % 2, a, :], late[a][0][:, :, piece_cols(b)], late[a][1][:, :, piece_cols(b)])
+        def pair_sum(engine, i):
+            for e in range(2):
+                late_sum(engine, 0, 2 * i + e, pairs[i][:, e, :])
 
-        def tail_quantise(start, count):
-            rounded = h_tail[start // 2][:, start % 2 : start % 2 + count].rearrange("p b a x -> p (b a x)")
-            codes, plane = h_operand("h_late%d" % start, rounded, count * PASSES * PIECE)
-            for i in range(count):
-                tail_features(start + i, codes, plane, i * PASSES * PIECE)
+        def pair_pass(i):
+            h_op = quantise("h_late0_mx%d" % i, pairs[i][:].rearrange("p e x -> p (e x)"))
+            for e in range(2):
+                piece_pass(0, 2 * i + e, columns(h_op, PIECE * e, PIECE))
 
-        def tail_features(b, codes, plane, at):
-            acc = psum.tile([P, N // P, PIECE], F32, name="acc_piece", tag="prod", bufs=6)
-            halves = [slice(at + PIECE * a, at + PIECE * (a + 1)) for a in range(PASSES)]
-            for n in range(N // P):
-                last_product(acc[:, n, :], n, [(codes[:, x], plane[:, x]) for x in halves], slice(0, PIECE))
-            res = keep.tile([P, N // P, PIECE], F32, name="res_piece%d" % b)
-            if b in TAIL_ON_VECTOR:
-                nc.vector.tensor_tensor(
-                    res[:], acc[:], bo_cols[:].unsqueeze(2).to_broadcast([P, N // P, PIECE]), ALU.add
-                )
+        def finish_piece(b):
+            piece_pass(1, b, quantise("h_late1_mx%d" % b, singles[b][:]))
+            res = keep.tile([P, OUT_TILES, PIECE], F32, name="res_piece%d" % b)
+            if b < PIECES - 1:
+                for n in range(OUT_TILES):
+                    add_bo_on_scalar(res[:, n, :], banks[b][:, n, :], n)
             else:
-                for n in range(N // P):
-                    nc.scalar.activation(res[:, n, :], acc[:, n, :], ACT.Identity, bias=bo_cols[:, n : n + 1])
-            nc.sync.dma_start(out_rows[:, :, piece_cols(b, BANK)], res[:])
+                bo_wide = bo_cols[:].unsqueeze(2).to_broadcast([P, OUT_TILES, PIECE])
+                nc.vector.tensor_tensor(res[:], banks[b][:], bo_wide, ALU.add)
+            nc.sync.dma_start(out_rows[:, :, BANK + PIECE * b : BANK + PIECE * (b + 1)], res[:])
 
-        tail_sum(0, 0)
-        tail_sum(0, 1)
-        tail_sum(1, 0)
-        tail_sum(1, 1)
-        tail_sum(0, 2)
-        tail_quantise(0, 2)
-        tail_sum(1, 2)
-        tail_sum(0, 3)
-        tail_quantise(2, 1)
-        tail_sum(1, 3)
-        tail_quantise(3, 1)
+        pair_sum(nc.gpsimd, 0)
+        pair_pass(0)
+        pair_sum(nc.vector, 1)
+        late_sum(nc.vector, 1, 0, singles[0][:])
+        pair_pass(1)
+        for b in range(1, PIECES):
+            late_sum(nc.vector, 1, b, singles[b][:])
+            finish_piece(b - 1)
+        finish_piece(PIECES - 1)

@@ -50,9 +50,13 @@ def tile_list_compound_gate_features_kernel(
         bg_cols = keep.tile([P, PASSES, PACK], F32, name="bg_cols")
         bo_cols = keep.tile([P, OUT_TILES], F32, name="bo_cols")
 
+        nc.vector.memset(wm_loaded_plane[:].bitcast(I32), 0)
         nc.vector.memset(table_plane[:].bitcast(I32), 0)
-        nc.gpsimd.memset(wm_loaded_plane[:].bitcast(I32), 0)
         nc.gpsimd.memset(wo_plane[:].rearrange("p a c -> p (a c)").bitcast(I32), 0)
+
+        warm = keep.tile([P, 2], F32, name="warm")
+        nc.gpsimd.memset(warm[:, 0:1], 0.0)
+        nc.scalar.activation(warm[:, 1:2], warm[:, 0:1], ACT.Sigmoid)
 
         def load_plane(plane, rows):
             for q in range(QUADRANTS):
@@ -63,16 +67,16 @@ def tile_list_compound_gate_features_kernel(
             nc.sync.dma_start(raw[:], w[:, BANK * a : BANK * (a + 1)].rearrange("(p i) c -> p i c", i=PACK))
             return raw
 
-        nc.sync.dma_start(table_words[:].bitcast(I32), tab_words[0].bitcast(I32))
         nc.sync.dma_start(mod_list[:], offs)
         nc.sync.dma_start(head_list[:], offs2)
+        load_plane(wm_loaded_plane, wm_scales[0])
         load_plane(table_plane, tab_scales[0])
+        nc.sync.dma_start(bg_cols[:], bg.rearrange("(a p t) -> p a t", a=PASSES, t=PACK))
+        nc.sync.dma_start(table_words[:].bitcast(I32), tab_words[0].bitcast(I32))
         wg_raw = [load_float_weight(wg, 0, "wg_raw0")]
         wh_raw = [load_float_weight(wh, 0, "wh_raw0")]
         wg_raw.append(load_float_weight(wg, 1, "wg_raw1"))
         nc.sync.dma_start(wm_loaded_words[:], wm_words[0].rearrange("p c i -> p (c i)").bitcast(I32))
-        load_plane(wm_loaded_plane, wm_scales[0])
-        nc.sync.dma_start(bg_cols[:], bg.rearrange("(a p t) -> p a t", a=PASSES, t=PACK))
         wh_raw.append(load_float_weight(wh, 1, "wh_raw1"))
         nc.sync.dma_start(wo_codes[:].bitcast(I32), wo_words.rearrange("a p c -> p a c").bitcast(I32))
         load_plane(wo_plane, wo_scales.rearrange("a q c -> q a c"))
@@ -102,26 +106,24 @@ def tile_list_compound_gate_features_kernel(
                 nc.scalar.activation(dst[:, :, :, t : t + 2], src[:, :, :, t : t + 2], ACT.Copy, scale=sign)
             return quantise(name, rounded[:])
 
-        def reorder_wm():
-            words = keep.tile([P, H], U32, name="wm_words", align_bytes=64)
-            plane = keep.tile([P, H], U8, name="wm_plane", align_bytes=64)
-            nc.vector.tensor_copy(
-                words[:].bitcast(I32).rearrange("p (a t m e) -> p a m t e", a=PASSES, t=PACK, e=2),
-                wm_loaded_words[:].rearrange("p (a m e t) -> p a m t e", a=PASSES, t=PACK, e=2),
-            )
-            nc.vector.tensor_copy(
-                plane[:].rearrange("p (a t m) -> p a t m", a=PASSES, t=PACK),
-                wm_loaded_plane[:].rearrange("p (a m t) -> p a t m", a=PASSES, t=PACK),
-            )
-            return words[:], plane[:]
+        wm_plane = keep.tile([P, H], U8, name="wm_plane", align_bytes=64)
+        nc.vector.tensor_copy(
+            wm_plane[:].rearrange("p (a t m) -> p a t m", a=PASSES, t=PACK),
+            wm_loaded_plane[:].rearrange("p (a m t) -> p a t m", a=PASSES, t=PACK),
+        )
+        mod_plane = gather("mod_plane", table_plane[:], mod_list)
+        head_plane = gather("head_plane", table_plane[:], head_list)
+        v_mod = gather("mod_words", table_words[:], mod_list), mod_plane
+        v_head = gather("head_words", table_words[:], head_list), head_plane
 
-        mod_words = gather("mod_words", table_words[:], mod_list)
-        head_words = gather("head_words", table_words[:], head_list)
-        v_mod = mod_words, gather("mod_plane", table_plane[:], mod_list)
-        v_head = head_words, gather("head_plane", table_plane[:], head_list)
         wg_ops = [quantise_weight("wg0", wg_raw[0], 1.0)]
         less_wh_ops = [quantise_weight("wh0", wh_raw[0], -1.0)]
-        wm_all = reorder_wm()
+        wm_codes = keep.tile([P, H], U32, name="wm_codes", align_bytes=64)
+        nc.vector.tensor_copy(
+            wm_codes[:].bitcast(I32).rearrange("p (a t m e) -> p a m t e", a=PASSES, t=PACK, e=2),
+            wm_loaded_words[:].rearrange("p (a m e t) -> p a m t e", a=PASSES, t=PACK, e=2),
+        )
+        wm_all = wm_codes[:], wm_plane[:]
         wm_ops = [columns(wm_all, BANK * a, BANK) for a in range(PASSES)]
         wg_ops.append(quantise_weight("wg1", wg_raw[1], 1.0))
         less_wh_ops.append(quantise_weight("wh1", wh_raw[1], -1.0))
@@ -209,7 +211,7 @@ def tile_list_compound_gate_features_kernel(
         h_early = keep.tile([P, PASSES, PIECES, PACK * PIECE], BF16, name="h_early", tag="wh1_round", align_bytes=64)
         terms = term_tiles()
         for t in range(PACK):
-            unit_terms(0, 0, t, terms, repeat=(t == PACK - 1))
+            unit_terms(0, 0, t, terms)
         for b in range(PIECES):
             add_and_round(nc.gpsimd, h_early[:, 0, b, :], piece_of(terms[0], b), piece_of(terms[1], b))
 
@@ -228,7 +230,7 @@ def tile_list_compound_gate_features_kernel(
             unit_terms(0, 1, t, late[0], lend_to="h_early_words" if t == half - 1 else None)
         early = quantise("h_early", h_early[:].rearrange("p a b x -> p (a b x)"))
         for t in range(half, PACK):
-            unit_terms(0, 1, t, late[0], repeat=(t == PACK - 1))
+            unit_terms(0, 1, t, late[0], repeat=True)
         for t in range(PACK):
             unit_terms(1, 1, t, late[1], lend_to="h_late0_1" if t == PACK - 1 else None)
 

from contextlib import ExitStack

import concourse.mybir as mybir

K, H, N, T, S = 512, 1024, 512, 4096, 1024
FLOPS = 3 * 2 * K * H * S + 2 * H * N * S

F32 = mybir.dt.float32
BF16 = mybir.dt.bfloat16
I32 = mybir.dt.int32
U32 = mybir.dt.uint32
U16 = mybir.dt.uint16
U8 = mybir.dt.uint8
FP8X4 = mybir.dt.float8_e4m3fn_x4
FP4X4 = mybir.dt.float4_e2m1fn_x4
ACT = mybir.ActivationFunctionType
ALU = mybir.AluOpType

P = 128
PACK = 4
QUADRANTS = 4
BANK = 512
PIECE = BANK // PACK
PIECES = BANK // PIECE
PASSES = H // (P * PACK)
OUT_TILES = N // P
GATE_BANKS = 2
SUM_BANKS = 6
GATE_TILES = 8


def tile_list_compound_gate_features_kernel(
    tc, tab_words, tab_scales, offs, offs2, wg, bg, wm_words, wm_scales, wh, wo_words, wo_scales, bo, out
):
    nc = tc.nc
    with ExitStack() as ctx:
        lists = ctx.enter_context(tc.tile_pool(name="lists", bufs=1))
        keep = ctx.enter_context(tc.tile_pool(name="keep", bufs=1))
        work = ctx.enter_context(tc.tile_pool(name="work", bufs=3))
        psum = ctx.enter_context(tc.psum_pool(name="psum", bufs=SUM_BANKS))

        mod_list = lists.tile([P, S // 16], U16, name="mod_list")
        head_list = lists.tile([P, S // 16], U16, name="head_list")
        table_words = keep.tile([P, T], U16, name="table_words", align_bytes=64)
        table_plane = keep.tile([P, T], U8, name="table_plane", align_bytes=64)
        wm_loaded_words = keep.tile([P, H], I32, name="wm_loaded_words")
        wm_loaded_plane = keep.tile([P, H], U8, name="wm_loaded_plane", align_bytes=64)
        wo_codes = keep.tile([P, PASSES, 2 * N], U8, name="wo_codes", align_bytes=64)
        wo_plane = keep.tile([P, PASSES, N], U8, name="wo_plane", align_bytes=64)
        bg_cols = keep.tile([P, PASSES, PACK], F32, name="bg_cols")
        bo_cols = keep.tile([P, OUT_TILES], F32, name="bo_cols")

        nc.vector.memset(wm_loaded_plane[:].bitcast(I32), 0)
        nc.vector.memset(table_plane[:].bitcast(I32), 0)
        nc.gpsimd.memset(wo_plane[:].rearrange("p a c -> p (a c)").bitcast(I32), 0)

        warm = keep.tile([P, 2], F32, name="warm")
        nc.gpsimd.memset(warm[:, 0:1], 0.0)
        nc.scalar.activation(warm[:, 1:2], warm[:, 0:1], ACT.Sigmoid)

        def load_plane(plane, rows):
            for q in range(QUADRANTS):
                nc.sync.dma_start(plane[32 * q : 32 * q + 4].bitcast(I32), rows[4 * q : 4 * q + 4].bitcast(I32))

        def load_float_weight(w, a, name):
            raw = keep.tile([P, PACK, BANK], F32, name=name)
            nc.sync.dma_start(raw[:], w[:, BANK * a : BANK * (a + 1)].rearrange("(p i) c -> p i c", i=PACK))
            return raw

        nc.sync.dma_start(mod_list[:], offs)
        nc.sync.dma_start(head_list[:], offs2)
        load_plane(wm_loaded_plane, wm_scales[0])
        load_plane(table_plane, tab_scales[0])
        nc.sync.dma_start(bg_cols[:], bg.rearrange("(a p t) -> p a t", a=PASSES, t=PACK))
        nc.sync.dma_start(table_words[:].bitcast(I32), tab_words[0].bitcast(I32))
        wg_raw = [load_float_weight(wg, 0, "wg_raw0")]
        wh_raw = [load_float_weight(wh, 0, "wh_raw0")]
        wg_raw.append(load_float_weight(wg, 1, "wg_raw1"))
        nc.sync.dma_start(wm_loaded_words[:], wm_words[0].rearrange("p c i -> p (c i)").bitcast(I32))
        wh_raw.append(load_float_weight(wh, 1, "wh_raw1"))
        nc.sync.dma_start(wo_codes[:].bitcast(I32), wo_words.rearrange("a p c -> p a c").bitcast(I32))
        load_plane(wo_plane, wo_scales.rearrange("a q c -> q a c"))
        with nc.allow_non_contiguous_dma(reason="bo lies one value a partition for each output tile"):
            nc.sync.dma_start(bo_cols[:], bo.rearrange("(n p) -> p n", p=P))

        def columns(operand, start, width):
            return operand[0][:, start : start + width], operand[1][:, start : start + width]

        def gather(name, table, offsets):
            picked = keep.tile([P, S], table.dtype, name=name, align_bytes=64)
            nc.vector.tensor_copy(picked[:], table.indirect(offsets[:]))
            return picked[:]

        def quantise(name, rounded):
            width = rounded.shape[1] // PACK
            words = keep.tile([P, width], U32, name=name + "_words", tag=name + "_words", align_bytes=64)
            plane = keep.tile([P, width], U8, name=name + "_plane", align_bytes=64)
            nc.vector.quantize_mx(out=words[:].bitcast(FP8X4), scales=plane[:], in_=rounded)
            return words[:], plane[:]

        def quantise_weight(name, raw, sign):
            rounded = keep.tile([P, BANK * PACK], BF16, name=name + "_round", tag=name + "_round", align_bytes=64)
            dst = rounded[:].rearrange("p (t m i) -> p m i t", t=PACK, i=PACK)
            src = raw[:].rearrange("p i (m t) -> p m i t", t=PACK)
            for t in range(0, PACK, 2):
                nc.scalar.activation(dst[:, :, :, t : t + 2], src[:, :, :, t : t + 2], ACT.Copy, scale=sign)
            return quantise(name, rounded[:])

        wm_plane = keep.tile([P, H], U8, name="wm_plane", align_bytes=64)
        nc.vector.tensor_copy(
            wm_plane[:].rearrange("p (a t m) -> p a t m", a=PASSES, t=PACK),
            wm_loaded_plane[:].rearrange("p (a m t) -> p a t m", a=PASSES, t=PACK),
        )
        mod_plane = gather("mod_plane", table_plane[:], mod_list)
        head_plane = gather("head_plane", table_plane[:], head_list)
        v_mod = gather("mod_words", table_words[:], mod_list), mod_plane
        v_head = gather("head_words", table_words[:], head_list), head_plane

        wg_ops = [quantise_weight("wg0", wg_raw[0], 1.0)]
        less_wh_ops = [quantise_weight("wh0", wh_raw[0], -1.0)]
        wm_codes = keep.tile([P, H], U32, name="wm_codes", align_bytes=64)
        nc.vector.tensor_copy(
            wm_codes[:].bitcast(I32).rearrange("p (a t m e) -> p a m t e", a=PASSES, t=PACK, e=2),
            wm_loaded_words[:].rearrange("p (a m e t) -> p a m t e", a=PASSES, t=PACK, e=2),
        )
        wm_all = wm_codes[:], wm_plane[:]
        wm_ops = [columns(wm_all, BANK * a, BANK) for a in range(PASSES)]
        wg_ops.append(quantise_weight("wg1", wg_raw[1], 1.0))
        less_wh_ops.append(quantise_weight("wh1", wh_raw[1], -1.0))

        def product(dst, weight, t, v, start_col, width, start=True, stop=True):
            lhs, rhs = columns(weight, P * t, P), columns(v, start_col, width)
            nc.tensor.matmul_mx(
                out=dst,
                lhsT=lhs[0].bitcast(FP8X4),
                lhsT_scale=lhs[1],
                rhs=rhs[0].bitcast(FP4X4),
                rhs_scale=rhs[1],
                start=start,
                stop=stop,
            )

        def sum_bank(shape, name):
            return psum.tile(shape, F32, name=name, tag="sums")

        def gate_of(a, c, t, lend_to):
            pre = psum.tile([P, BANK], F32, name="pre", tag="pre", bufs=GATE_BANKS)
            product(pre[:], wg_ops[a], t, v_mod, BANK * c, BANK)
            if lend_to:
                gate = keep.tile([P, BANK], F32, name="lent_gate", tag=lend_to, align_bytes=64)
            else:
                gate = work.tile([P, BANK], F32, name="gate", tag="gate", bufs=GATE_TILES)
            nc.scalar.activation(gate[:], pre[:], ACT.Sigmoid, bias=bg_cols[:, a, t : t + 1])
            return gate

        def gate_less_one_times(dst, gate, bank):
            nc.vector.scalar_tensor_tensor(dst, gate[:], 1.0, bank[:], ALU.subtract, ALU.mult)

        def mod_less_head(a, c, t):
            bank = sum_bank([P, BANK], "mod_less_head")
            product(bank[:], wm_ops[a], t, v_mod, BANK * c, BANK, stop=False)
            product(bank[:], less_wh_ops[a], t, v_head, BANK * c, BANK, start=False)
            return bank

        def term_tiles():
            return (
                work.tile([P, PACK, BANK], F32, name="first", tag="first"),
                work.tile([P, PACK, BANK], F32, name="second", tag="second"),
            )

        def unit_terms(a, c, t, terms, repeat=False, lend_to=None):
            gate = gate_of(a, c, t, lend_to)
            mod = sum_bank([P, BANK], "mod")
            product(mod[:], wm_ops[a], t, v_mod, BANK * c, BANK)
            if repeat:
                other = mod_less_head(a, c, t)
                nc.scalar.copy(terms[0][:, t, :], mod[:])
            else:
                other = sum_bank([P, BANK], "less_head")
                product(other[:], less_wh_ops[a], t, v_head, BANK * c, BANK)
                nc.vector.tensor_tensor(terms[0][:, t, :], gate[:], mod[:], ALU.mult)
            gate_less_one_times(terms[1][:, t, :], gate, other)

        def piece_of(term, b):
            return term[:, :, PIECE * b : PIECE * (b + 1)]

        def add_and_round(engine, dst, first, second):
            engine.tensor_tensor(
                dst.rearrange("p (c e t) -> p c t e", e=2, t=PACK),
                first.rearrange("p t (c e) -> p c t e", e=2),
                second.rearrange("p t (c e) -> p c t e", e=2),
                ALU.add,
            )

        out_rows = out.rearrange("(n p) j -> p n j", p=P)

        def last_pass(dst, n, a, h_op, start, stop):
            nc.tensor.matmul_mx(
                out=dst,
                lhsT=wo_codes[:, a, 2 * P * n : 2 * P * (n + 1)].bitcast(FP4X4),
                lhsT_scale=wo_plane[:, a, P * n : P * (n + 1)],
                rhs=h_op[0].bitcast(FP8X4),
                rhs_scale=h_op[1],
                start=start,
                stop=stop,
            )

        def add_bo_on_scalar(dst, acc, n):
            nc.scalar.activation(dst, acc, ACT.Identity, bias=bo_cols[:, n : n + 1])

        h_early = keep.tile([P, PASSES, PIECES, PACK * PIECE], BF16, name="h_early", tag="wh1_round", align_bytes=64)
        terms = term_tiles()
        for t in range(PACK):
            unit_terms(0, 0, t, terms)
        for b in range(PIECES):
            add_and_round(nc.gpsimd, h_early[:, 0, b, :], piece_of(terms[0], b), piece_of(terms[1], b))

        scaled = work.tile([P, PACK, BANK], F32, name="scaled", tag="second")
        for t in range(PACK):
            gate_less_one_times(scaled[:, t, :], gate_of(1, 0, t, None), mod_less_head(1, 0, t))
        for b in range(PIECES):
            mod = sum_bank([P, PACK, PIECE], "mod_piece")
            for t in range(PACK):
                product(mod[:, t, :], wm_ops[1], t, v_mod, PIECE * b, PIECE)
            add_and_round(nc.vector, h_early[:, 1, b, :], piece_of(scaled, b), mod[:])

        late = [term_tiles(), term_tiles()]
        half = PACK // 2
        for t in range(half):
            unit_terms(0, 1, t, late[0], lend_to="h_early_words" if t == half - 1 else None)
        early = quantise("h_early", h_early[:].rearrange("p a b x -> p (a b x)"))
        for t in range(half, PACK):
            unit_terms(0, 1, t, late[0], repeat=True)
        for t in range(PACK):
            unit_terms(1, 1, t, late[1], lend_to="h_late0_1" if t == PACK - 1 else None)

        for n in range(OUT_TILES):
            acc = sum_bank([P, BANK], "acc")
            for a in range(PASSES):
                last_pass(acc[:], n, a, columns(early, BANK * a, BANK), a == 0, a == PASSES - 1)
            res = work.tile([P, BANK], F32, name="res", tag="res", bufs=OUT_TILES)
            add_bo_on_scalar(res[:], acc[:], n)
            nc.sync.dma_start(out_rows[:, n, 0:BANK], res[:])

        banks = [sum_bank([P, OUT_TILES, PIECE], "acc_piece%d" % b) for b in range(PIECES)]

        def late_sum(engine, a, b, dst):
            add_and_round(engine, dst, piece_of(late[a][0], b), piece_of(late[a][1], b))

        def piece_pass(a, b, h_op):
            for n in range(OUT_TILES):
                last_pass(banks[b][:, n, :], n, a, h_op, a == 0 and n == 0, a == PASSES - 1 and n == OUT_TILES - 1)

        pairs = [
            keep.tile([P, 2, PACK * PIECE], BF16, name="h_late0_%d" % i, tag="h_late0_%d" % i, align_bytes=64)
            for i in range(PIECES // 2)
        ]
        singles = [keep.tile([P, PACK * PIECE], BF16, name="h_late1_%d" % b, align_bytes=64) for b in range(PIECES)]

        def pair_sum(engine, i):
            for e in range(2):
                late_sum(engine, 0, 2 * i + e, pairs[i][:, e, :])

        def pair_pass(i):
            h_op = quantise("h_late0_mx%d" % i, pairs[i][:].rearrange("p e x -> p (e x)"))
            for e in range(2):
                piece_pass(0, 2 * i + e, columns(h_op, PIECE * e, PIECE))

        def finish_piece(b):
            piece_pass(1, b, quantise("h_late1_mx%d" % b, singles[b][:]))
            res = keep.tile([P, OUT_TILES, PIECE], F32, name="res_piece%d" % b)
            if b < PIECES - 1:
                for n in range(OUT_TILES):
                    add_bo_on_scalar(res[:, n, :], banks[b][:, n, :], n)
            else:
                bo_wide = bo_cols[:].unsqueeze(2).to_broadcast([P, OUT_TILES, PIECE])
                nc.vector.tensor_tensor(res[:], banks[b][:], bo_wide, ALU.add)
            nc.sync.dma_start(out_rows[:, :, BANK + PIECE * b : BANK + PIECE * (b + 1)], res[:])

        pair_sum(nc.gpsimd, 0)
        pair_pass(0)
        pair_sum(nc.vector, 1)
        late_sum(nc.vector, 1, 0, singles[0][:])
        pair_pass(1)
        for b in range(1, PIECES):
            late_sum(nc.vector, 1, b, singles[b][:])
            finish_piece(b - 1)
        finish_piece(PIECES - 1)
